import numpy as np
import ml_dtypes


def mxq(x, axis, fmt="e4m3"):
    dtype, down = {"e4m3": (ml_dtypes.float8_e4m3fn, 7), "e5m2": (ml_dtypes.float8_e5m2, 14)}[fmt]
    v = np.moveaxis(np.asarray(x, np.float32).astype(ml_dtypes.bfloat16).astype(np.float64), axis, -1)
    blocks = v.reshape(v.shape[:-1] + (-1, 32))
    amax = np.abs(blocks).max(-1, keepdims=True)
    byte = np.maximum(np.where(amax > 0, np.frexp(amax)[1] - 1 + 127, 0) - down, 1)
    scale = np.exp2(byte - 127.0)
    codes = (blocks / scale).astype(np.float32).astype(dtype).astype(np.float64)
    return np.moveaxis((codes * scale).reshape(v.shape), -1, axis)


WIDE = False


def mx_kscale(k):
    if not WIDE:
        return np.ones(k)
    levels = np.array([10, -10, 5, -5, 0])
    if k % 512:
        return np.exp2(np.random.permutation(np.resize(levels, k // 32))).repeat(32)
    a = np.empty((k // 512, 16))
    for p in range(k // 512):
        a[p, :8] = np.random.permutation(np.resize(levels, 8))
        for g in range(8):
            far = levels[np.abs(levels - a[p, g]) >= 10]
            a[p, g + 8] = far[np.random.randint(len(far))]
    return np.exp2(a.ravel()).repeat(32)


def f64(x):
    return np.asarray(x).astype(np.float64)


def striped(idx):
    return np.tile(idx.reshape(-1, 16).T, (8, 1)).astype(np.uint16)


def unstriped(offs):
    return offs[:16].T.reshape(-1).astype(np.int64)


def pack_weight(w):
    k, n = w.shape
    w = f64(np.asarray(w, np.float32).astype(ml_dtypes.bfloat16)).reshape(k // 32, 32, n)
    amax = np.abs(w).max(1)
    byte = np.clip(np.where(amax > 0, np.frexp(amax)[1] - 1 + 127 - 7, 1), 1, 254)
    scaled = (w * np.exp2(127.0 - byte)[:, None, :]).reshape(k, n).astype(np.float32)
    words = np.ascontiguousarray(scaled.reshape(k // 512, 128, 4, n).transpose(0, 1, 3, 2)).astype(ml_dtypes.float8_e4m3fn).view(np.uint8)
    return words, np.ascontiguousarray(byte.astype(np.uint8).reshape(k // 512, 16, n))


def unpack_weight(words, scales):
    g, p, n, _ = words.shape
    vals = np.ascontiguousarray(words).view(ml_dtypes.float8_e4m3fn).astype(np.float64) * np.repeat(np.exp2(scales.astype(np.float64) - 127.0), 8, axis=1)[..., None]
    return vals.transpose(0, 1, 3, 2).reshape(g * 512, n)


K, T, E, C, N = 1536, 2048, 16, 128, 128


def by_expert(wq, xq):
    return np.concatenate([wq[e].T @ xq[:, e * C:(e + 1) * C] for e in range(E)], axis=1)


def setup_inputs():
    n = np.random.standard_normal
    s = mx_kscale(K)[:, None]
    packed = [pack_weight(m) for m in n((E, K, N)) / np.sqrt(K) / s[None]]
    return {
        "xT": (n((K, T)) * s).astype(np.float32),
        "w_words": np.stack([m[0] for m in packed]),
        "w_scales": np.stack([m[1] for m in packed]),
        "gate": np.tile(np.random.uniform(0.2, 1.0, E * C), (N, 1)).astype(np.float32),
        "offs": striped(np.random.permutation(T)[:E * C]),
    }


def reference(xT, w_words, w_scales, gate, offs):
    idx = unstriped(offs)
    xq = mxq(f64(xT)[:, idx], 0, "e4m3")
    w = np.stack([unpack_weight(w_words[e], w_scales[e]) for e in range(E)])
    y = by_expert(w, xq)
    out = np.zeros((N, T))
    out[:, idx] = f64(gate) * y
    return out

@@ -1,0 +1,130 @@
+from contextlib import ExitStack
+
+import concourse.mybir as mybir
+
+K, T, E, C, N = 1536, 2048, 16, 128, 128
+FLOPS = 2 * K * N * E * C
+
+F32 = mybir.dt.float32
+BF16 = mybir.dt.bfloat16
+U32 = mybir.dt.uint32
+I32 = mybir.dt.int32
+U16 = mybir.dt.uint16
+U8 = mybir.dt.uint8
+FP8X4 = mybir.dt.float8_e4m3fn_x4
+MULT = mybir.AluOpType.mult
+
+P = 128
+PACK = 4
+K_PASS = P * PACK
+PASSES = K // K_PASS
+BANK = 512
+CHUNKS = [(a, c, 512) for a in range(PASSES) for c in range(0, T, 512)][:-1] + [(2, 1536, 256), (2, 1792, 256)]
+GROUPS = [(0, 1024, True), (1024, 512, True), (1536, 512, False)]
+VECTOR_CHUNKS = (0, 3, 7)
+
+
+def interleave(copy, grouped, raw, c0, c1):
+    copy(
+        out=grouped[:, c0:c1, :].rearrange("p (c i) t -> p c t i", i=4),
+        in_=raw[:, :, c0:c1].rearrange("p t (c i) -> p c t i", i=4),
+    )
+
+
+def tile_routed_moe_kernel(tc, xT, w_words, w_scales, gate, offs, out):
+    nc = tc.nc
+    with ExitStack() as ctx:
+        keep = ctx.enter_context(tc.tile_pool(name="keep", bufs=1))
+        rawp = ctx.enter_context(tc.tile_pool(name="rawp", bufs=8))
+        grpp = ctx.enter_context(tc.tile_pool(name="grpp", bufs=4))
+        yp = ctx.enter_context(tc.tile_pool(name="yp", bufs=2))
+        psum = ctx.enter_context(tc.psum_pool(name="psum", bufs=4))
+
+        lists = keep.tile([P, T // 16], U16, name="lists")
+        words = [keep.tile([P, T], U32, name=f"words{a}", align_bytes=64) for a in range(PASSES)]
+        got_words = [keep.tile([P, T], U32, name=f"got_words{a}", align_bytes=64) for a in range(PASSES)]
+        scales = keep.tile([P, T], U8, name="scales", align_bytes=64)
+        got_scales = keep.tile([P, T], U8, name="got_scales", align_bytes=64)
+        w_sb = keep.tile([P, E * PASSES, N], U32, name="w_sb", align_bytes=64)
+        ws_sb = keep.tile([P, E * PASSES, N], U8, name="ws_sb", align_bytes=64)
+        gate_sb = keep.tile([P, T], F32, name="gate_sb")
+        out_sb = keep.tile([P, T], F32, name="out_sb")
+
+        nc.gpsimd.memset(scales[:], 0)
+        nc.vector.memset(ws_sb[:].rearrange("p a n -> p (a n)").bitcast(I32), 0)
+
+        x_view = xT.rearrange("(a p t) n -> a p t n", p=P, t=PACK)
+        raws = []
+        for i, (a, c, n) in enumerate(CHUNKS):
+            raw = rawp.tile([P, PACK, n], F32, name="raw")
+            nc.sync.dma_start(out=raw[:], in_=x_view[a, :, :, c : c + n])
+            raws.append(raw)
+            if i == 1:
+                nc.sync.dma_start(lists[:], offs)
+
+        ws_view = w_scales.bitcast(I32).rearrange("e a q m -> q (e a) m")
+        for q in range(4):
+            nc.sync.dma_start(out=ws_sb[32 * q : 32 * q + 4, :, :].bitcast(I32), in_=ws_view[4 * q : 4 * q + 4, :, :])
+        w_view = w_words.rearrange("e a p n r -> e a p (n r)").bitcast(I32).rearrange("e a p m -> p (e a) m")
+        for lo, n, on_gpsimd in GROUPS:
+            rows = slice(lo // C * PASSES, (lo + n) // C * PASSES)
+            nc.sync.dma_start(out=w_sb[:, rows, :].bitcast(I32), in_=w_view[:, rows, :])
+            nc.sync.dma_start(out=gate_sb[:, lo : lo + n], in_=gate[:, lo : lo + n])
+
+        def offsets(lo, n):
+            return lists[:, lo // 16 : (lo + n) // 16]
+
+        def gather_words(a, lo, n):
+            nc.vector.tensor_copy(got_words[a][:, lo : lo + n], words[a][:].indirect(offsets(lo, n)))
+
+        def gather_scales(lo, n):
+            nc.vector.tensor_copy(got_scales[:, lo : lo + n], scales[:].indirect(offsets(lo, n)))
+
+        for i, (a, c, n) in enumerate(CHUNKS):
+            cols = slice(c, c + n)
+            grouped = grpp.tile([P, n, PACK], BF16, name="grouped", align_bytes=64)
+            if i in VECTOR_CHUNKS:
+                interleave(nc.vector.tensor_copy, grouped, raws[i], 0, n)
+            elif i == len(CHUNKS) - 1:
+                interleave(nc.scalar.copy, grouped, raws[i], 0, n // 2)
+                interleave(nc.vector.tensor_copy, grouped, raws[i], n // 2, n)
+            else:
+                interleave(nc.scalar.copy, grouped, raws[i], 0, n)
+            nc.vector.quantize_mx(
+                out=words[a][:, cols].bitcast(FP8X4),
+                scales=scales[4 * a : P, cols],
+                in_=grouped[:].rearrange("p c t -> p (c t)"),
+            )
+            if c + n == T and a < PASSES - 1:
+                for lo in range(0, T, 1024):
+                    gather_words(a, lo, 1024)
+
+        for lo, n, on_gpsimd in GROUPS:
+            gather_words(PASSES - 1, lo, n)
+            gather_scales(lo, n)
+        for lo, n, on_gpsimd in GROUPS:
+            y = keep.tile([P, n], F32, name=f"y{lo}")
+            for b in range(lo, lo + n, BANK):
+                acc = psum.tile([P, BANK], F32, name="acc")
+                for j in range(BANK // C):
+                    e = b // C + j
+                    slots = slice(e * C, (e + 1) * C)
+                    for a in range(PASSES):
+                        nc.tensor.matmul_mx(
+                            out=acc[:, j * C : (j + 1) * C],
+                            lhsT=w_sb[:, e * PASSES + a, :].bitcast(FP8X4),
+                            lhsT_scale=ws_sb[:, e * PASSES + a, :],
+                            rhs=got_words[a][:, slots].bitcast(FP8X4),
+                            rhs_scale=got_scales[4 * a : P, slots],
+                            start=(a == 0),
+                            stop=(a == PASSES - 1),
+                        )
+                part = y[:, b - lo : b - lo + BANK]
+                if on_gpsimd:
+                    sums = yp.tile([P, BANK], F32, name="sums")
+                    nc.scalar.copy(out=sums[:], in_=acc[:])
+                    nc.gpsimd.tensor_tensor(out=part, in0=sums[:], in1=gate_sb[:, b : b + BANK], op=MULT)
+                else:
+                    nc.vector.tensor_tensor(out=part, in0=acc[:], in1=gate_sb[:, b : b + BANK], op=MULT)
+            nc.vector.tensor_copy(out_sb[:].indirect(offsets(lo, n)), y[:])
+        nc.sync.dma_start(out=out, in_=out_sb[:])

@@ -18,16 +18,18 @@ P = 128
 PACK = 4
 K_PASS = P * PACK
 PASSES = K // K_PASS
-BANK = 512
-CHUNKS = [(a, c, 512) for a in range(PASSES) for c in range(0, T, 512)][:-1] + [(2, 1536, 256), (2, 1792, 256)]
-GROUPS = [(0, 1024, True), (1024, 512, True), (1536, 512, False)]
-VECTOR_CHUNKS = (0, 3, 7)
+PIECE = 512
+LOADS = [(0, 0, 1024), (0, 1024, 1024), (1, 0, 1024), (1, 1024, 1024), (2, 0, 1024), (2, 1024, 512), (2, 1536, 512)]
+VECTOR_PIECES = (0, 2, 5, 8)
+LAST_SPLIT = 192
+GATHER = 1024
+GROUP = 512
 
 
-def interleave(copy, grouped, raw, c0, c1):
+def interleave(copy, grouped, raw, g0, r0, n):
     copy(
-        out=grouped[:, c0:c1, :].rearrange("p (c i) t -> p c t i", i=4),
-        in_=raw[:, :, c0:c1].rearrange("p t (c i) -> p c t i", i=4),
+        out=grouped[:, g0 : g0 + n, :].rearrange("p (c i) t -> p c t i", i=4),
+        in_=raw[:, :, r0 : r0 + n].rearrange("p t (c i) -> p c t i", i=4),
     )
 
 
@@ -35,9 +37,8 @@ def tile_routed_moe_kernel(tc, xT, w_words, w_scales, gate, offs, out):
     nc = tc.nc
     with ExitStack() as ctx:
         keep = ctx.enter_context(tc.tile_pool(name="keep", bufs=1))
-        rawp = ctx.enter_context(tc.tile_pool(name="rawp", bufs=8))
-        grpp = ctx.enter_context(tc.tile_pool(name="grpp", bufs=4))
-        yp = ctx.enter_context(tc.tile_pool(name="yp", bufs=2))
+        grpp = ctx.enter_context(tc.tile_pool(name="grpp", bufs=5))
+        yp = ctx.enter_context(tc.tile_pool(name="yp", bufs=3))
         psum = ctx.enter_context(tc.psum_pool(name="psum", bufs=4))
 
         lists = keep.tile([P, T // 16], U16, name="lists")
@@ -54,22 +55,23 @@ def tile_routed_moe_kernel(tc, xT, w_words, w_scales, gate, offs, out):
         nc.vector.memset(ws_sb[:].rearrange("p a n -> p (a n)").bitcast(I32), 0)
 
         x_view = xT.rearrange("(a p t) n -> a p t n", p=P, t=PACK)
-        raws = []
-        for i, (a, c, n) in enumerate(CHUNKS):
-            raw = rawp.tile([P, PACK, n], F32, name="raw")
+        pieces = []
+        for i, (a, c, n) in enumerate(LOADS):
+            raw = keep.tile([P, PACK, n], F32, name=f"raw{i}")
             nc.sync.dma_start(out=raw[:], in_=x_view[a, :, :, c : c + n])
-            raws.append(raw)
-            if i == 1:
+            if i == 0:
                 nc.sync.dma_start(lists[:], offs)
+            for r in range(0, n, PIECE):
+                pieces.append((a, c + r, raw, r))
 
         ws_view = w_scales.bitcast(I32).rearrange("e a q m -> q (e a) m")
         for q in range(4):
             nc.sync.dma_start(out=ws_sb[32 * q : 32 * q + 4, :, :].bitcast(I32), in_=ws_view[4 * q : 4 * q + 4, :, :])
         w_view = w_words.rearrange("e a p n r -> e a p (n r)").bitcast(I32).rearrange("e a p m -> p (e a) m")
-        for lo, n, on_gpsimd in GROUPS:
-            rows = slice(lo // C * PASSES, (lo + n) // C * PASSES)
+        for lo in range(0, T, GROUP):
+            rows = slice(lo // C * PASSES, (lo + GROUP) // C * PASSES)
             nc.sync.dma_start(out=w_sb[:, rows, :].bitcast(I32), in_=w_view[:, rows, :])
-            nc.sync.dma_start(out=gate_sb[:, lo : lo + n], in_=gate[:, lo : lo + n])
+            nc.sync.dma_start(out=gate_sb[:, lo : lo + GROUP], in_=gate[:, lo : lo + GROUP])
 
         def offsets(lo, n):
             return lists[:, lo // 16 : (lo + n) // 16]
@@ -80,51 +82,44 @@ def tile_routed_moe_kernel(tc, xT, w_words, w_scales, gate, offs, out):
         def gather_scales(lo, n):
             nc.vector.tensor_copy(got_scales[:, lo : lo + n], scales[:].indirect(offsets(lo, n)))
 
-        for i, (a, c, n) in enumerate(CHUNKS):
-            cols = slice(c, c + n)
-            grouped = grpp.tile([P, n, PACK], BF16, name="grouped", align_bytes=64)
-            if i in VECTOR_CHUNKS:
-                interleave(nc.vector.tensor_copy, grouped, raws[i], 0, n)
-            elif i == len(CHUNKS) - 1:
-                interleave(nc.scalar.copy, grouped, raws[i], 0, n // 2)
-                interleave(nc.vector.tensor_copy, grouped, raws[i], n // 2, n)
+        for i, (a, c, raw, r) in enumerate(pieces):
+            cols = slice(c, c + PIECE)
+            grouped = grpp.tile([P, PIECE, PACK], BF16, name="grouped", align_bytes=64)
+            if i in VECTOR_PIECES:
+                interleave(nc.vector.tensor_copy, grouped, raw, 0, r, PIECE)
+            elif i == len(pieces) - 1:
+                interleave(nc.scalar.copy, grouped, raw, 0, r, LAST_SPLIT)
+                interleave(nc.vector.tensor_copy, grouped, raw, LAST_SPLIT, r + LAST_SPLIT, PIECE - LAST_SPLIT)
             else:
-                interleave(nc.scalar.copy, grouped, raws[i], 0, n)
+                interleave(nc.scalar.copy, grouped, raw, 0, r, PIECE)
             nc.vector.quantize_mx(
                 out=words[a][:, cols].bitcast(FP8X4),
                 scales=scales[4 * a : P, cols],
                 in_=grouped[:].rearrange("p c t -> p (c t)"),
             )
-            if c + n == T and a < PASSES - 1:
-                for lo in range(0, T, 1024):
-                    gather_words(a, lo, 1024)
+            if c + PIECE == T and a < PASSES - 1:
+                for lo in range(0, T, GATHER):
+                    gather_words(a, lo, GATHER)
 
-        for lo, n, on_gpsimd in GROUPS:
-            gather_words(PASSES - 1, lo, n)
-            gather_scales(lo, n)
-        for lo, n, on_gpsimd in GROUPS:
-            y = keep.tile([P, n], F32, name=f"y{lo}")
-            for b in range(lo, lo + n, BANK):
-                acc = psum.tile([P, BANK], F32, name="acc")
-                for j in range(BANK // C):
-                    e = b // C + j
-                    slots = slice(e * C, (e + 1) * C)
-                    for a in range(PASSES):
-                        nc.tensor.matmul_mx(
-                            out=acc[:, j * C : (j + 1) * C],
-                            lhsT=w_sb[:, e * PASSES + a, :].bitcast(FP8X4),
-                            lhsT_scale=ws_sb[:, e * PASSES + a, :],
-                            rhs=got_words[a][:, slots].bitcast(FP8X4),
-                            rhs_scale=got_scales[4 * a : P, slots],
-                            start=(a == 0),
-                            stop=(a == PASSES - 1),
-                        )
-                part = y[:, b - lo : b - lo + BANK]
-                if on_gpsimd:
-                    sums = yp.tile([P, BANK], F32, name="sums")
-                    nc.scalar.copy(out=sums[:], in_=acc[:])
-                    nc.gpsimd.tensor_tensor(out=part, in0=sums[:], in1=gate_sb[:, b : b + BANK], op=MULT)
-                else:
-                    nc.vector.tensor_tensor(out=part, in0=acc[:], in1=gate_sb[:, b : b + BANK], op=MULT)
-            nc.vector.tensor_copy(out_sb[:].indirect(offsets(lo, n)), y[:])
+        for lo in range(0, T, GATHER):
+            gather_words(PASSES - 1, lo, GATHER)
+            gather_scales(lo, GATHER)
+        for lo in range(0, T, GROUP):
+            acc = psum.tile([P, GROUP], F32, name="acc")
+            for j in range(GROUP // C):
+                e = lo // C + j
+                slots = slice(e * C, (e + 1) * C)
+                for a in range(PASSES):
+                    nc.tensor.matmul_mx(
+                        out=acc[:, j * C : (j + 1) * C],
+                        lhsT=w_sb[:, e * PASSES + a, :].bitcast(FP8X4),
+                        lhsT_scale=ws_sb[:, e * PASSES + a, :],
+                        rhs=got_words[a][:, slots].bitcast(FP8X4),
+                        rhs_scale=got_scales[4 * a : P, slots],
+                        start=(a == 0),
+                        stop=(a == PASSES - 1),
+                    )
+            y = yp.tile([P, GROUP], F32, name="y")
+            nc.scalar.copy(out=y[:], in_=acc[:])
+            nc.vector.tensor_tensor(out_sb[:].indirect(offsets(lo, GROUP)), y[:], gate_sb[:, lo : lo + GROUP], MULT)
         nc.sync.dma_start(out=out, in_=out_sb[:])

@@ -19,11 +19,11 @@ PACK = 4
 K_PASS = P * PACK
 PASSES = K // K_PASS
 PIECE = 512
-LOADS = [(0, 0, 1024), (0, 1024, 1024), (1, 0, 1024), (1, 1024, 1024), (2, 0, 1024), (2, 1024, 512), (2, 1536, 512)]
-VECTOR_PIECES = (0, 2, 5, 8)
-LAST_SPLIT = 192
+LOADS = [(a, c, 512) for a in range(PASSES) for c in range(0, T, 512)]
+VECTOR_TOKENS = (512, 512, 512, 256) + (0,) * 7 + (256,)
 GATHER = 1024
-GROUP = 512
+BANK = 512
+GROUP = 1024
 
 
 def interleave(copy, grouped, raw, g0, r0, n):
@@ -38,7 +38,7 @@ def tile_routed_moe_kernel(tc, xT, w_words, w_scales, gate, offs, out):
     with ExitStack() as ctx:
         keep = ctx.enter_context(tc.tile_pool(name="keep", bufs=1))
         grpp = ctx.enter_context(tc.tile_pool(name="grpp", bufs=5))
-        yp = ctx.enter_context(tc.tile_pool(name="yp", bufs=3))
+        yp = ctx.enter_context(tc.tile_pool(name="yp", bufs=2))
         psum = ctx.enter_context(tc.psum_pool(name="psum", bufs=4))
 
         lists = keep.tile([P, T // 16], U16, name="lists")
@@ -68,10 +68,10 @@ def tile_routed_moe_kernel(tc, xT, w_words, w_scales, gate, offs, out):
         for q in range(4):
             nc.sync.dma_start(out=ws_sb[32 * q : 32 * q + 4, :, :].bitcast(I32), in_=ws_view[4 * q : 4 * q + 4, :, :])
         w_view = w_words.rearrange("e a p n r -> e a p (n r)").bitcast(I32).rearrange("e a p m -> p (e a) m")
-        for lo in range(0, T, GROUP):
-            rows = slice(lo // C * PASSES, (lo + GROUP) // C * PASSES)
+        for lo in range(0, T, BANK):
+            rows = slice(lo // C * PASSES, (lo + BANK) // C * PASSES)
             nc.sync.dma_start(out=w_sb[:, rows, :].bitcast(I32), in_=w_view[:, rows, :])
-            nc.sync.dma_start(out=gate_sb[:, lo : lo + GROUP], in_=gate[:, lo : lo + GROUP])
+            nc.sync.dma_start(out=gate_sb[:, lo : lo + BANK], in_=gate[:, lo : lo + BANK])
 
         def offsets(lo, n):
             return lists[:, lo // 16 : (lo + n) // 16]
@@ -83,20 +83,20 @@ def tile_routed_moe_kernel(tc, xT, w_words, w_scales, gate, offs, out):
             nc.vector.tensor_copy(got_scales[:, lo : lo + n], scales[:].indirect(offsets(lo, n)))
 
         for i, (a, c, raw, r) in enumerate(pieces):
-            cols = slice(c, c + PIECE)
             grouped = grpp.tile([P, PIECE, PACK], BF16, name="grouped", align_bytes=64)
-            if i in VECTOR_PIECES:
-                interleave(nc.vector.tensor_copy, grouped, raw, 0, r, PIECE)
-            elif i == len(pieces) - 1:
-                interleave(nc.scalar.copy, grouped, raw, 0, r, LAST_SPLIT)
-                interleave(nc.vector.tensor_copy, grouped, raw, LAST_SPLIT, r + LAST_SPLIT, PIECE - LAST_SPLIT)
-            else:
-                interleave(nc.scalar.copy, grouped, raw, 0, r, PIECE)
-            nc.vector.quantize_mx(
-                out=words[a][:, cols].bitcast(FP8X4),
-                scales=scales[4 * a : P, cols],
-                in_=grouped[:].rearrange("p c t -> p (c t)"),
-            )
+            v = VECTOR_TOKENS[i]
+            if v > 0:
+                interleave(nc.vector.tensor_copy, grouped, raw, 0, r, v)
+            if v < PIECE:
+                interleave(nc.scalar.copy, grouped, raw, v, r + v, PIECE - v)
+            step = PIECE // 2 if i == len(pieces) - 1 else PIECE
+            for o in range(0, PIECE, step):
+                cols = slice(c + o, c + o + step)
+                nc.vector.quantize_mx(
+                    out=words[a][:, cols].bitcast(FP8X4),
+                    scales=scales[4 * a : P, cols],
+                    in_=grouped[:, o : o + step, :].rearrange("p c t -> p (c t)"),
+                )
             if c + PIECE == T and a < PASSES - 1:
                 for lo in range(0, T, GATHER):
                     gather_words(a, lo, GATHER)
@@ -105,21 +105,22 @@ def tile_routed_moe_kernel(tc, xT, w_words, w_scales, gate, offs, out):
             gather_words(PASSES - 1, lo, GATHER)
             gather_scales(lo, GATHER)
         for lo in range(0, T, GROUP):
-            acc = psum.tile([P, GROUP], F32, name="acc")
-            for j in range(GROUP // C):
-                e = lo // C + j
-                slots = slice(e * C, (e + 1) * C)
-                for a in range(PASSES):
-                    nc.tensor.matmul_mx(
-                        out=acc[:, j * C : (j + 1) * C],
-                        lhsT=w_sb[:, e * PASSES + a, :].bitcast(FP8X4),
-                        lhsT_scale=ws_sb[:, e * PASSES + a, :],
-                        rhs=got_words[a][:, slots].bitcast(FP8X4),
-                        rhs_scale=got_scales[4 * a : P, slots],
-                        start=(a == 0),
-                        stop=(a == PASSES - 1),
-                    )
             y = yp.tile([P, GROUP], F32, name="y")
-            nc.scalar.copy(out=y[:], in_=acc[:])
+            for b in range(0, GROUP, BANK):
+                acc = psum.tile([P, BANK], F32, name="acc")
+                for j in range(BANK // C):
+                    e = (lo + b) // C + j
+                    slots = slice(e * C, (e + 1) * C)
+                    for a in range(PASSES):
+                        nc.tensor.matmul_mx(
+                            out=acc[:, j * C : (j + 1) * C],
+                            lhsT=w_sb[:, e * PASSES + a, :].bitcast(FP8X4),
+                            lhsT_scale=ws_sb[:, e * PASSES + a, :],
+                            rhs=got_words[a][:, slots].bitcast(FP8X4),
+                            rhs_scale=got_scales[4 * a : P, slots],
+                            start=(a == 0),
+                            stop=(a == PASSES - 1),
+                        )
+                nc.scalar.copy(out=y[:, b : b + BANK], in_=acc[:])
             nc.vector.tensor_tensor(out_sb[:].indirect(offsets(lo, GROUP)), y[:], gate_sb[:, lo : lo + GROUP], MULT)
         nc.sync.dma_start(out=out, in_=out_sb[:])

@@ -19,11 +19,11 @@ PACK = 4
 K_PASS = P * PACK
 PASSES = K // K_PASS
 PIECE = 512
-LOADS = [(a, c, 512) for a in range(PASSES) for c in range(0, T, 512)]
-VECTOR_TOKENS = (512, 512, 512, 256) + (0,) * 7 + (256,)
+LOADS = [(0, 0, 1024), (0, 1024, 1024), (1, 0, 1024), (1, 1024, 1024), (2, 0, 512), (2, 512, 512), (2, 1024, 512), (2, 1536, 256), (2, 1792, 256)]
+VECTOR_TOKENS = (512, 0, 512, 0, 0, 128, 512, 0, 0, 0, 256, 0, 128)
 GATHER = 1024
 BANK = 512
-GROUP = 1024
+GROUPS = [(0, 512), (512, 512), (1024, 1024)]
 
 
 def interleave(copy, grouped, raw, g0, r0, n):
@@ -62,7 +62,7 @@ def tile_routed_moe_kernel(tc, xT, w_words, w_scales, gate, offs, out):
             if i == 0:
                 nc.sync.dma_start(lists[:], offs)
             for r in range(0, n, PIECE):
-                pieces.append((a, c + r, raw, r))
+                pieces.append((a, c + r, raw, r, min(PIECE, n)))
 
         ws_view = w_scales.bitcast(I32).rearrange("e a q m -> q (e a) m")
         for q in range(4):
@@ -82,31 +82,29 @@ def tile_routed_moe_kernel(tc, xT, w_words, w_scales, gate, offs, out):
         def gather_scales(lo, n):
             nc.vector.tensor_copy(got_scales[:, lo : lo + n], scales[:].indirect(offsets(lo, n)))
 
-        for i, (a, c, raw, r) in enumerate(pieces):
-            grouped = grpp.tile([P, PIECE, PACK], BF16, name="grouped", align_bytes=64)
+        for i, (a, c, raw, r, n) in enumerate(pieces):
+            grouped = grpp.tile([P, n, PACK], BF16, name="grouped", align_bytes=64)
             v = VECTOR_TOKENS[i]
             if v > 0:
                 interleave(nc.vector.tensor_copy, grouped, raw, 0, r, v)
-            if v < PIECE:
-                interleave(nc.scalar.copy, grouped, raw, v, r + v, PIECE - v)
-            step = PIECE // 2 if i == len(pieces) - 1 else PIECE
-            for o in range(0, PIECE, step):
-                cols = slice(c + o, c + o + step)
-                nc.vector.quantize_mx(
-                    out=words[a][:, cols].bitcast(FP8X4),
-                    scales=scales[4 * a : P, cols],
-                    in_=grouped[:, o : o + step, :].rearrange("p c t -> p (c t)"),
-                )
-            if c + PIECE == T and a < PASSES - 1:
+            if v < n:
+                interleave(nc.scalar.copy, grouped, raw, v, r + v, n - v)
+            cols = slice(c, c + n)
+            nc.vector.quantize_mx(
+                out=words[a][:, cols].bitcast(FP8X4),
+                scales=scales[4 * a : P, cols],
+                in_=grouped[:].rearrange("p c t -> p (c t)"),
+            )
+            if c + n == T and a < PASSES - 1:
                 for lo in range(0, T, GATHER):
                     gather_words(a, lo, GATHER)
 
         for lo in range(0, T, GATHER):
             gather_words(PASSES - 1, lo, GATHER)
             gather_scales(lo, GATHER)
-        for lo in range(0, T, GROUP):
-            y = yp.tile([P, GROUP], F32, name="y")
-            for b in range(0, GROUP, BANK):
+        for lo, n in GROUPS:
+            y = yp.tile([P, n], F32, name="y")
+            for b in range(0, n, BANK):
                 acc = psum.tile([P, BANK], F32, name="acc")
                 for j in range(BANK // C):
                     e = (lo + b) // C + j
@@ -122,5 +120,5 @@ def tile_routed_moe_kernel(tc, xT, w_words, w_scales, gate, offs, out):
                             stop=(a == PASSES - 1),
                         )
                 nc.scalar.copy(out=y[:, b : b + BANK], in_=acc[:])
-            nc.vector.tensor_tensor(out_sb[:].indirect(offsets(lo, GROUP)), y[:], gate_sb[:, lo : lo + GROUP], MULT)
+            nc.vector.tensor_tensor(out_sb[:].indirect(offsets(lo, n)), y[:], gate_sb[:, lo : lo + n], MULT)
         nc.sync.dma_start(out=out, in_=out_sb[:])

@@ -23,7 +23,6 @@ LOADS = [(0, 0, 1024), (0, 1024, 1024), (1, 0, 1024), (1, 1024, 1024), (2, 0, 51
 VECTOR_TOKENS = (512, 0, 512, 0, 0, 128, 512, 0, 0, 0, 256, 0, 128)
 GATHER = 1024
 BANK = 512
-GROUPS = [(0, 512), (512, 512), (1024, 1024)]
 
 
 def interleave(copy, grouped, raw, g0, r0, n):
@@ -38,7 +37,7 @@ def tile_routed_moe_kernel(tc, xT, w_words, w_scales, gate, offs, out):
     with ExitStack() as ctx:
         keep = ctx.enter_context(tc.tile_pool(name="keep", bufs=1))
         grpp = ctx.enter_context(tc.tile_pool(name="grpp", bufs=5))
-        yp = ctx.enter_context(tc.tile_pool(name="yp", bufs=2))
+        yp = ctx.enter_context(tc.tile_pool(name="yp", bufs=4))
         psum = ctx.enter_context(tc.psum_pool(name="psum", bufs=4))
 
         lists = keep.tile([P, T // 16], U16, name="lists")
@@ -68,10 +67,15 @@ def tile_routed_moe_kernel(tc, xT, w_words, w_scales, gate, offs, out):
         for q in range(4):
             nc.sync.dma_start(out=ws_sb[32 * q : 32 * q + 4, :, :].bitcast(I32), in_=ws_view[4 * q : 4 * q + 4, :, :])
         w_view = w_words.rearrange("e a p n r -> e a p (n r)").bitcast(I32).rearrange("e a p m -> p (e a) m")
-        for lo in range(0, T, BANK):
+        def load_weights(lo):
             rows = slice(lo // C * PASSES, (lo + BANK) // C * PASSES)
             nc.sync.dma_start(out=w_sb[:, rows, :].bitcast(I32), in_=w_view[:, rows, :])
+
+        def load_gate(lo):
             nc.sync.dma_start(out=gate_sb[:, lo : lo + BANK], in_=gate[:, lo : lo + BANK])
+
+        for load, lo in [(load_weights, 0), (load_gate, 0), (load_weights, 512), (load_gate, 512), (load_weights, 1024), (load_weights, 1536), (load_gate, 1024), (load_gate, 1536)]:
+            load(lo)
 
         def offsets(lo, n):
             return lists[:, lo // 16 : (lo + n) // 16]
@@ -102,23 +106,22 @@ def tile_routed_moe_kernel(tc, xT, w_words, w_scales, gate, offs, out):
         for lo in range(0, T, GATHER):
             gather_words(PASSES - 1, lo, GATHER)
             gather_scales(lo, GATHER)
-        for lo, n in GROUPS:
-            y = yp.tile([P, n], F32, name="y")
-            for b in range(0, n, BANK):
-                acc = psum.tile([P, BANK], F32, name="acc")
-                for j in range(BANK // C):
-                    e = (lo + b) // C + j
-                    slots = slice(e * C, (e + 1) * C)
-                    for a in range(PASSES):
-                        nc.tensor.matmul_mx(
-                            out=acc[:, j * C : (j + 1) * C],
-                            lhsT=w_sb[:, e * PASSES + a, :].bitcast(FP8X4),
-                            lhsT_scale=ws_sb[:, e * PASSES + a, :],
-                            rhs=got_words[a][:, slots].bitcast(FP8X4),
-                            rhs_scale=got_scales[4 * a : P, slots],
-                            start=(a == 0),
-                            stop=(a == PASSES - 1),
-                        )
-                nc.scalar.copy(out=y[:, b : b + BANK], in_=acc[:])
-            nc.vector.tensor_tensor(out_sb[:].indirect(offsets(lo, n)), y[:], gate_sb[:, lo : lo + n], MULT)
+        for lo in range(0, T, BANK):
+            acc = psum.tile([P, BANK], F32, name="acc")
+            for j in range(BANK // C):
+                e = lo // C + j
+                slots = slice(e * C, (e + 1) * C)
+                for a in range(PASSES):
+                    nc.tensor.matmul_mx(
+                        out=acc[:, j * C : (j + 1) * C],
+                        lhsT=w_sb[:, e * PASSES + a, :].bitcast(FP8X4),
+                        lhsT_scale=ws_sb[:, e * PASSES + a, :],
+                        rhs=got_words[a][:, slots].bitcast(FP8X4),
+                        rhs_scale=got_scales[4 * a : P, slots],
+                        start=(a == 0),
+                        stop=(a == PASSES - 1),
+                    )
+            y = yp.tile([P, BANK], F32, name="y")
+            nc.scalar.copy(out=y[:], in_=acc[:])
+            nc.vector.tensor_tensor(out_sb[:].indirect(offsets(lo, BANK)), y[:], gate_sb[:, lo : lo + BANK], MULT)
         nc.sync.dma_start(out=out, in_=out_sb[:])

from contextlib import ExitStack

import concourse.mybir as mybir

K, T, E, C, N = 1536, 2048, 16, 128, 128
FLOPS = 2 * K * N * E * C

F32 = mybir.dt.float32
BF16 = mybir.dt.bfloat16
U32 = mybir.dt.uint32
I32 = mybir.dt.int32
U16 = mybir.dt.uint16
U8 = mybir.dt.uint8
FP8X4 = mybir.dt.float8_e4m3fn_x4
MULT = mybir.AluOpType.mult

P = 128
PACK = 4
K_PASS = P * PACK
PASSES = K // K_PASS
PIECE = 512
LOADS = [(0, 0, 1024), (0, 1024, 1024), (1, 0, 1024), (1, 1024, 1024), (2, 0, 512), (2, 512, 512), (2, 1024, 512), (2, 1536, 256), (2, 1792, 256)]
VECTOR_TOKENS = (512, 0, 512, 0, 0, 128, 512, 0, 0, 0, 256, 0, 128)
GATHER = 1024
BANK = 512


def interleave(copy, grouped, raw, g0, r0, n):
    copy(
        out=grouped[:, g0 : g0 + n, :].rearrange("p (c i) t -> p c t i", i=4),
        in_=raw[:, :, r0 : r0 + n].rearrange("p t (c i) -> p c t i", i=4),
    )


def tile_routed_moe_kernel(tc, xT, w_words, w_scales, gate, offs, out):
    nc = tc.nc
    with ExitStack() as ctx:
        keep = ctx.enter_context(tc.tile_pool(name="keep", bufs=1))
        grpp = ctx.enter_context(tc.tile_pool(name="grpp", bufs=5))
        yp = ctx.enter_context(tc.tile_pool(name="yp", bufs=4))
        psum = ctx.enter_context(tc.psum_pool(name="psum", bufs=4))

        lists = keep.tile([P, T // 16], U16, name="lists")
        words = [keep.tile([P, T], U32, name=f"words{a}", align_bytes=64) for a in range(PASSES)]
        got_words = [keep.tile([P, T], U32, name=f"got_words{a}", align_bytes=64) for a in range(PASSES)]
        scales = keep.tile([P, T], U8, name="scales", align_bytes=64)
        got_scales = keep.tile([P, T], U8, name="got_scales", align_bytes=64)
        w_sb = keep.tile([P, E * PASSES, N], U32, name="w_sb", align_bytes=64)
        ws_sb = keep.tile([P, E * PASSES, N], U8, name="ws_sb", align_bytes=64)
        gate_sb = keep.tile([P, T], F32, name="gate_sb")
        out_sb = keep.tile([P, T], F32, name="out_sb")

        nc.gpsimd.memset(scales[:], 0)
        nc.vector.memset(ws_sb[:].rearrange("p a n -> p (a n)").bitcast(I32), 0)

        x_view = xT.rearrange("(a p t) n -> a p t n", p=P, t=PACK)
        pieces = []
        for i, (a, c, n) in enumerate(LOADS):
            raw = keep.tile([P, PACK, n], F32, name=f"raw{i}")
            nc.sync.dma_start(out=raw[:], in_=x_view[a, :, :, c : c + n])
            if i == 0:
                nc.sync.dma_start(lists[:], offs)
            for r in range(0, n, PIECE):
                pieces.append((a, c + r, raw, r, min(PIECE, n)))

        ws_view = w_scales.bitcast(I32).rearrange("e a q m -> q (e a) m")
        for q in range(4):
            nc.sync.dma_start(out=ws_sb[32 * q : 32 * q + 4, :, :].bitcast(I32), in_=ws_view[4 * q : 4 * q + 4, :, :])
        w_view = w_words.rearrange("e a p n r -> e a p (n r)").bitcast(I32).rearrange("e a p m -> p (e a) m")
        def load_weights(lo):
            rows = slice(lo // C * PASSES, (lo + BANK) // C * PASSES)
            nc.sync.dma_start(out=w_sb[:, rows, :].bitcast(I32), in_=w_view[:, rows, :])

        def load_gate(lo):
            nc.sync.dma_start(out=gate_sb[:, lo : lo + BANK], in_=gate[:, lo : lo + BANK])

        for load, lo in [(load_weights, 0), (load_gate, 0), (load_weights, 512), (load_gate, 512), (load_weights, 1024), (load_weights, 1536), (load_gate, 1024), (load_gate, 1536)]:
            load(lo)

        def offsets(lo, n):
            return lists[:, lo // 16 : (lo + n) // 16]

        def gather_words(a, lo, n):
            nc.vector.tensor_copy(got_words[a][:, lo : lo + n], words[a][:].indirect(offsets(lo, n)))

        def gather_scales(lo, n):
            nc.vector.tensor_copy(got_scales[:, lo : lo + n], scales[:].indirect(offsets(lo, n)))

        for i, (a, c, raw, r, n) in enumerate(pieces):
            grouped = grpp.tile([P, n, PACK], BF16, name="grouped", align_bytes=64)
            v = VECTOR_TOKENS[i]
            if v > 0:
                interleave(nc.vector.tensor_copy, grouped, raw, 0, r, v)
            if v < n:
                interleave(nc.scalar.copy, grouped, raw, v, r + v, n - v)
            cols = slice(c, c + n)
            nc.vector.quantize_mx(
                out=words[a][:, cols].bitcast(FP8X4),
                scales=scales[4 * a : P, cols],
                in_=grouped[:].rearrange("p c t -> p (c t)"),
            )
            if c + n == T and a < PASSES - 1:
                for lo in range(0, T, GATHER):
                    gather_words(a, lo, GATHER)

        for lo in range(0, T, GATHER):
            gather_words(PASSES - 1, lo, GATHER)
            gather_scales(lo, GATHER)
        for lo in range(0, T, BANK):
            acc = psum.tile([P, BANK], F32, name="acc")
            for j in range(BANK // C):
                e = lo // C + j
                slots = slice(e * C, (e + 1) * C)
                for a in range(PASSES):
                    nc.tensor.matmul_mx(
                        out=acc[:, j * C : (j + 1) * C],
                        lhsT=w_sb[:, e * PASSES + a, :].bitcast(FP8X4),
                        lhsT_scale=ws_sb[:, e * PASSES + a, :],
                        rhs=got_words[a][:, slots].bitcast(FP8X4),
                        rhs_scale=got_scales[4 * a : P, slots],
                        start=(a == 0),
                        stop=(a == PASSES - 1),
                    )
            y = yp.tile([P, BANK], F32, name="y")
            nc.scalar.copy(out=y[:], in_=acc[:])
            nc.vector.tensor_tensor(out_sb[:].indirect(offsets(lo, BANK)), y[:], gate_sb[:, lo : lo + BANK], MULT)
        nc.sync.dma_start(out=out, in_=out_sb[:])
